import numpy as np, ml_dtypes
CORES = [40,41,42,43,44,45,46,47]
N = 8
import mx_ref
BF = ml_dtypes.bfloat16
def cols(t, e):
    v = np.concatenate([t.reshape(128, -1, 4), np.zeros((128, 1, 4), BF)], axis=1)
    return np.ascontiguousarray(v[:, e]).reshape(128, -1)
def decode(q):
    o = []
    for b in range(4):
        e = np.zeros((128, 128, 4), np.float32); e[np.arange(128), np.arange(128), b] = 1
        o.append(mx_ref.matmul(mx_ref.quantize(e.reshape(128, 512).astype(BF)), q))
    return np.stack(o, axis=2).reshape(128, -1)
def f(rng, *shape):
    return mx_ref.flush((rng.standard_normal(shape, dtype=np.float32) * np.exp2(rng.integers(-2, 3, shape[:-1] + (1,)))).astype(BF))
def wide(rng, *shape, cols=0):
    v = rng.standard_normal(shape, dtype=np.float32) * np.exp2(rng.integers(-12, 13, shape)).astype(np.float32)
    if cols: v *= np.repeat(np.exp2(rng.integers(-cols, cols + 1, shape[:-2] + (1, shape[-1] // 4))) * (rng.random(shape[:-2] + (1, shape[-1] // 4)) > 0.0625), 4, axis=-1).astype(np.float32)
    return mx_ref.flush(v.astype(BF))
K = 384
def plant(t, k, v):
    o = t.astype(np.float32).reshape(128, -1, 4); o[:, k] = v
    return o.reshape(128, -1).astype(BF)
def setup_inputs(rng):
    return {"x": f(rng, N, 128, 512), "c1": f(rng, N, 128, 4 * K), "c2": f(rng, N, 128, 4 * K)}
def setup_inputs_last(rng):
    d = setup_inputs(rng); u = f(rng, 128, 4).astype(np.float32).reshape(128, 1, 4); x = []
    s = np.exp2(np.where(np.arange(128) < 120, 2, 0) + np.arange(128) % 2).astype(np.float32).reshape(1, 128, 1)
    for r in range(N):
        x.append(plant(d["x"][r], rng.permutation(128), u * s))
    d["x"] = np.stack(x)
    for c in ("c1", "c2"):
        d[c] = np.stack([plant(d[c][q], [K - 1], np.float32(2) * u) if q == N - 1 else d[c][q] for q in range(N)])
    return d
def setup_inputs_negative(rng):
    d = setup_inputs(rng)
    for c, s in (("x", 1), ("c1", -1), ("c2", -1)):
        d[c] = (np.abs(d[c].astype(np.float32)) * np.float32(s * 2.0 ** 20)).astype(BF)
    return d
def setup_inputs_own(rng):
    d = setup_inputs(rng)
    for c, s in (("c1", 2), ("c2", -2)):
        d[c] = np.stack([plant(d[c][r], rng.permutation(K)[:128], np.float32(s) * d["x"][r].astype(np.float32).reshape(128, -1, 4)) for r in range(N)])
    return d
def setup_inputs_spread(rng):
    d = setup_inputs(rng); d["x"] = wide(rng, N, 128, 512, cols=8)
    for c in ("c1", "c2"): d[c] = wide(rng, N, 128, 4 * K, cols=2)
    return d
def setup_inputs_ties(rng):
    d = setup_inputs(rng)
    d["x"] = np.stack([plant(d["x"][r], rng.permutation(128)[:1], np.zeros((128, 1, 4), np.float32)) for r in range(N)])
    for c in ("c1", "c2"):
        a = f(rng, N, 128, K)
        d[c] = np.stack([cols(np.concatenate([a[q], a[q], a[(q + 1) % N], a[(q + 2) % N]], axis=1), rng.permutation(K)) for q in range(N)])
    return d
def check_inputs(d):
    b = []
    for c in ("x", "c1", "c2"):
        a = np.abs(d[c].astype(np.float32))
        if not (np.isfinite(a) & ((a == 0) | ((a >= 2.0 ** -30) & (a <= 2.0 ** 30)))).all(): b.append(c)
    return b
def winners(v, book):
    s = np.concatenate([mx_ref.matmul(v, q) for q in book], axis=1)
    w = np.argmax(s + np.float32(0), axis=1)
    return w, s[np.arange(128), w]
def chosen(t, e):
    return t.reshape(128, -1, 4)[:, e].reshape(128, -1)
def reference(x, c1, c2):
    q1 = [mx_ref.quantize(c1[q]) for q in range(N)]
    q2 = [mx_ref.quantize(c2[q]) for q in range(N)]
    d1 = np.concatenate([decode(q) for q in q1], axis=1)
    d2 = np.concatenate([decode(q) for q in q2], axis=1)
    y = np.zeros((N, 128, 512), np.float32); no = np.zeros((N, 4, 128), np.float32)
    for r in range(N):
        w1, s1 = winners(mx_ref.quantize(x[r]), q1)
        R = (x[r].astype(np.float32) - chosen(d1, w1)).astype(BF)
        w2, s2 = winners(mx_ref.quantize(R), q2)
        y[r] = R.astype(np.float32) - chosen(d2, w2)
        no[r, 0] = w1; no[r, 1] = w2; no[r, 2] = s1; no[r, 3] = s2
    return {"y": y, "no": no}

from concourse.bass import DstId, RemoteDMATransfer
from concourse.mybir import dt, AluOpType, AxisListType, ActivationFunctionType

N, K = 8, 384
W1 = K + 7 * 128
W2 = 4 * K + 4 * 128
BIG = 1000000.0
LOW = -9.0e29

F, B, C8, U8, I32, U16 = "float32", "bfloat16", "float8_e4m3fn_x4", "uint8", "int32", "uint16"


def sb(n, d):
    return ("sbuf", [128, n], d)


SCRATCH = {
    "xt": ("sbuf", [128, 64, 8], B), "xs": sb(512, B), "xv": sb(512, B), "c1t": sb(4 * K, B), "c2t": sb(4 * K, B),
    "c1p": sb(4 * K, B), "c2p": sb(4 * K, B),
    "ones": sb(128, B), "ident": sb(128, B), "et": sb(2048, B), "eqc": sb(512, C8), "eqs": sb(512, U8), "lim": sb(K, B),
    "xqc": sb(1024, C8), "xqs": sb(1024, U8), "rqc": sb(1024, C8), "rqs": sb(1024, U8),
    "q1c": sb(K, C8), "q1s": sb(K, U8), "q2c": sb(4 * K, C8), "q2s": sb(4 * K, U8),
    "run": sb(16 * K, F), "junk": sb(16 * K, B),
    "mia": sb(6, F), "mib": sb(8, F), "mic": sb(8, F), "cva": sb(48, F), "cvb": sb(64, F), "cvc": sb(64, F),
    "ofa": sb(24, U16), "ofb": sb(32, U16), "ofc": sb(32, U16),
    "gta": sb(1536, B), "gtb": sb(2048, B), "gtc": sb(2048, B),
    "sac": sb(384, C8), "sas": sb(384, U8), "sbc": sb(512, C8), "sbs": sb(512, U8), "scc": sb(512, C8), "scs": sb(512, U8),
    "kac": sb(384, C8), "kas": sb(384, U8), "kbc": sb(512, C8), "kbs": sb(512, U8), "kcc": sb(512, C8), "kcs": sb(512, U8),
    "sci1": sb(32, F), "sci2": sb(32, F), "tab1": sb(4 * W1, F), "tab2": sb(4 * W2, F),
    "pen1": sb(8, F), "pen2": sb(8, F), "tp1": sb(8, F), "tp2": sb(8, F), "tn1": sb(8, F), "tn2": sb(8, F),
    "pp1": sb(8, F), "pp2": sb(8, F), "nb": sb(8, F), "num1": sb(8, F), "num2": sb(8, F),
    "pos1": sb(1, F), "pos2": sb(1, F), "cvp1": sb(8, F), "cvp2": sb(8, F), "ofp1": sb(8, U16), "ofp2": sb(8, U16),
    "wp1": sb(32, F), "wt1": sb(32, F), "il": sb(256, F), "ou": sb(256, F), "wp2": sb(2, F), "nc": sb(32, F), "nct": sb(32, F),
    "pi": sb(1, I32), "ia": sb(1, I32), "ib": sb(1, I32), "iu": sb(1, I32), "it": sb(1, I32), "iw": sb(32, I32),
    "fa": sb(1, F), "fu": sb(1, F), "jv": sb(1, F), "ut": sb(1, F), "lrn": sb(32, U16),
    "rt": sb(512, B), "rn": sb(512, B), "yt": sb(512, F),
}
for _b in range(8):
    SCRATCH["p%d" % _b] = ("psum", [128, 512], F)
SEMAPHORES = (["pv", "ps", "pt", "pg", "ls", "lx", "lc1", "lc2", "cva", "cvb", "cvc", "cvp1", "cvp2", "il", "no1", "nc", "no2",
               "yo", "ac2", "as1", "as2", "aka", "akb", "akc"]
              + ["ax%d" % q for q in range(N)] + ["ar%d" % q for q in range(N)])


def rank_program(g, core, T, topo):
    me = T.rank_of(core)
    if me is None:
        return
    A, X, FN = AluOpType, AxisListType.X, ActivationFunctionType
    ranks = list(range(N))

    def same(a, b):
        return topo.die(T.cores[a]) == topo.die(T.cores[b])

    def home_of(r):
        return [q for q in ranks if same(q, r)]

    def mates_of(r):
        return [q for q in ranks if q != r and same(q, r)]

    def far_of(r):
        return [q for q in ranks if not same(q, r)]

    home, mates, far = home_of(me), mates_of(me), far_of(me)
    sem = T.sem
    queue = {"v": g.vector, "s": g.scalar, "t": g.tensor, "g": g, "y": g.sync}
    count, seen, local, total = {}, {}, [0], {}

    def need(qn, deps):
        top = {}
        for s, v in deps:
            top[s] = max(top.get(s, 0), v)
        for s in sorted(top):
            if seen.get((qn, s), 0) < top[s]:
                queue[qn].wait_ge(sem[s], top[s])
                seen[(qn, s)] = top[s]

    def did(name, ins):
        ins.then_inc(sem[name], 1)
        count[name] = count.get(name, 0) + 1
        return (name, count[name])

    def V(deps, call, *a, **k):
        need("v", deps)
        return did("pv", call(*a, **k))

    def S(deps, call, *a, **k):
        need("s", deps)
        return did("ps", call(*a, **k))

    def G(deps, call, *a, **k):
        need("g", deps)
        return did("pg", call(*a, **k))

    def D(qn, deps, name, out, in_):
        need(qn, deps)
        queue[qn].dma_start(out, in_).then_inc(sem[name], 16)
        total[name] = total.get(name, 0) + 16
        return (name, total[name])

    vec, act = g.vector, g.scalar.activation

    def send(deps, name, items):
        need("g", deps)
        n = 1
        while n < len(items):
            n *= 2
        tr = []
        for k, (dst, s, d) in enumerate(items):
            eng = topo.engines(core, T.cores[dst[0]])
            per = len(eng) // n
            mask = 0
            for e in eng[k * per:(k + 1) * per]:
                mask |= 1 << e
            ids = []
            for q in dst:
                rid, pid, _ = topo.addr(T.cores[q])
                ids.append(DstId(rid=rid, pnc=pid))
            tr.append(RemoteDMATransfer(dst_ids=ids, dma_engine_mask=mask, remote_sem=sem[name], srcs=[s], dsts=[d] * len(ids)))
            local[0] += per
        g.remote_dma_fused(tr, local_sem=sem.ls)

    def width(n):
        eng = len(topo.engines(core, T.cores[(me + 1) % N]))
        k = 1
        while k < n:
            k *= 2
        return eng // k

    def u8(t, a, b):
        return t[:, a:b].bitcast(dt.uint8)

    bank = [T["p%d" % b] for b in range(8)]
    free = [[] for _ in range(8)]

    def mm(b, n, lc, lsc, la, rc, rsc, ra, deps):
        need("t", deps + free[b])
        return did("pt", g.tensor.matmul_mx(bank[b][:, 0:n], lc[:, la:la + 128], lsc[:, la:la + 128],
                                            rc[:, ra:ra + n], rsc[:, ra:ra + n], True, True))

    def evac(qn, b, n, tab, w, t, runs, dep):
        tk = []
        for src, dst, m in runs:
            o, i = tab[:, t * w + dst:t * w + dst + m], bank[b][:, src:src + m]
            if qn == "v":
                tk.append(V([dep], vec.tensor_scalar, o, i, -1.0, None, A.mult))
            else:
                tk.append(S([dep], act, o, i, FN.Copy, scale=-1.0))
        free[b] = tk
        return tk

    base1, base2, a1, a2 = [], [], 0, 0
    for q in ranks:
        base1.append(a1)
        base2.append(a2)
        a1 += K if q == me else 128
        a2 += K if q in home else 128

    def runs_of(group, base):
        out = []
        for k, q in enumerate(group):
            if out and out[-1][1] + out[-1][2] == base[q]:
                out[-1] = (out[-1][0], out[-1][1], out[-1][2] + 128)
            else:
                out.append((128 * k, base[q], 128))
        return out

    dx = D("y", [], "lx", T.xt[:, :, :], T.x[:, :])
    d1 = D("s", [], "lc1", T.c1t[:, :], T.c1[:, :])
    d2 = D("y", [], "lc2", T.c2t[:, :], T.c2[:, :])

    o1 = V([], vec.memset, T.ones[:, :], 1.0)
    i1 = G([o1], g.affine_select, T.ident[:, :], T.ones[:, :], [[-1, 128]], A.is_equal, 0.0, 0, 1)
    i2 = G([], g.iota, T.pi[:, :], [[0, 1]], 0, 1)
    i3 = G([], g.iota, T.iw[:, :], [[4, 8], [128, 4]], 0, 0)
    i4 = G([], g.iota, T.nb[:, :], [[K, 8]], 0, 0, allow_small_or_imprecise_dtypes=True)
    ez = V([], vec.memset, T.et[:, :], 0.0)
    lm = V([], vec.memset, T.lim[:, :], LOW)

    u0 = V([dx], vec.tensor_copy, T.xs[:, 0:256], T.xt[:, :, 0:4])
    u1 = S([dx], act, T.xs[:, 256:512], T.xt[:, :, 4:8], FN.Copy)
    m0 = 128 * me
    qx = V([u0, u1], vec.quantize_mx, T.xqc[:, m0:m0 + 128], T.xqs[:, m0:m0 + 128], T.xs[:, :])
    others = mates + far
    send([qx], "ax%d" % me, [(others, u8(T.xqc, m0, m0 + 128), u8(T.xqc, m0, m0 + 128))])
    send([qx], "ax%d" % me, [(others, T.xqs[:, m0:m0 + 128], T.xqs[:, m0:m0 + 128])])

    ec = [V([i1, ez], vec.tensor_copy, T.et[:, 512 * b + b:512 * (b + 1):4], T.ident[:, :]) for b in range(4)]
    qe = V(ec, vec.quantize_mx, T.eqc[:, :], T.eqs[:, :], T.et[:, :])
    q1 = V([d1], vec.quantize_mx, T.q1c[:, :], T.q1s[:, :], T.c1t[:, :])
    pl1 = [V([d1], vec.tensor_copy, T.c1p[:, K * t:K * (t + 1)], T.c1t[:, t:4 * K:4]) for t in (0, 1)]

    ka = V([i2], vec.tensor_scalar, T.ia[:, :], T.pi[:, :], 7, None, A.bitwise_and)
    kb = V([i2], vec.tensor_scalar, T.ib[:, :], T.pi[:, :], 3, None, A.arith_shift_right)
    ku = V([i2], vec.tensor_scalar, T.iu[:, :], T.pi[:, :], 2, 3, A.arith_shift_right, A.bitwise_and)
    kt = V([i2], vec.tensor_scalar, T.it[:, :], T.pi[:, :], 3, None, A.bitwise_and)
    kf = V([ka], vec.tensor_scalar, T.fa[:, :], T.ia[:, :], 16.0, None, A.mult)
    kg = V([ku], vec.tensor_scalar, T.fu[:, :], T.iu[:, :], 32.0, None, A.mult)
    jv = V([kf, kb], vec.tensor_tensor, T.jv[:, :], T.fa[:, :], T.ib[:, :], A.add)
    kh = V([kg, kt], vec.tensor_tensor, T.ut[:, :], T.fu[:, :], T.it[:, :], A.add)
    lr = V([kh, i3], vec.tensor_scalar, T.lrn[:, :], T.iw[:, :], T.ut[:, :], None, A.add)

    pl1 += [S([d1], act, T.c1p[:, K * t:K * (t + 1)], T.c1t[:, t:4 * K:4], FN.Copy) for t in (2, 3)]

    score_no = [0]

    def scan(b, dep):
        k = score_no[0]
        score_no[0] += 1
        tk = V([dep, lm], vec.tensor_tensor_scan, T.run[:, K * k:K * (k + 1)], bank[b][:, 0:K], T.lim[:, :], LOW, A.max, A.max)
        free[b] = [tk]
        return k, tk

    def sign(k, tk, acc):
        return S([tk], act, T.junk[:, K * k:K * (k + 1)], T.run[:, K * k:K * (k + 1)], FN.Sign,
                 bias=T.run[:, K * (k + 1) - 1:K * (k + 1)], scale=-1.0, accum_out=acc)

    so = mm(4, K, T.xqc, T.xqs, m0, T.q1c, T.q1s, 0, [qx, q1])
    to = [mm(b, K, T.eqc, T.eqs, 128 * b, T.q1c, T.q1s, 0, [qe, q1]) for b in range(4)]
    k0, s0 = scan(4, so)
    n0 = sign(k0, s0, T.sci1[:, 4 * me + 1:4 * me + 2])
    ow = [V([s0], vec.tensor_copy, T.sci1[:, 4 * me:4 * me + 1], T.run[:, K * (k0 + 1) - 1:K * (k0 + 1)])]
    t1 = [[], [], [], []]
    for b in range(4):
        t1[b] += evac("v" if b < 2 else "s", b, K, T.tab1, W1, b, [(0, base1[me], K)], to[b])
    hm = K * home.index(me)
    q2 = V([d2], vec.quantize_mx, T.q2c[:, hm:hm + K], T.q2s[:, hm:hm + K], T.c2t[:, :])
    send([q2], "ac2", [(mates, u8(T.q2c, hm, hm + K), u8(T.q2c, hm, hm + K))])
    send([q2], "ac2", [(mates, T.q2s[:, hm:hm + K], T.q2s[:, hm:hm + K])])
    wz = V([], vec.memset, T.wp1[:, :], 0.0)
    nz = V([], vec.memset, T.nc[:, :], 0.0)
    p1 = []
    for q in others:
        p1.append(V([jv], vec.tensor_scalar, T.pp1[:, q:q + 1], T.jv[:, :], float(base1[q]), None, A.add))
    xv = S([u0, u1, lr], act, T.xv[:, :], T.xs[:, 0:512].indirect(T.lrn[:, 0:32]), FN.Copy)

    def score(group, banks, rc, rs, qc, qs, arrived, dw):
        return [mm(banks[i], K, rc, rs, 128 * q, qc, qs, dw, [arrived(q)]) for i, q in enumerate(group)]

    def search(group, banks, tks, mi):
        n = len(group)
        sc = [scan(banks[i], tks[i]) for i in range(n)]
        first = sc[0][0]
        mx = V([s for _, s in sc], vec.tensor_copy, mi[:, 0:2 * n:2], T.run[:, K * (first + 1) - 1:K * (first + n):K])
        sg = [sign(k, tk, mi[:, 2 * i + 1:2 * i + 2]) for i, (k, tk) in enumerate(sc)]
        return [mx] + sg

    def spread(name, src, dst, deps, queues):
        for k in range(8):
            D(queues[k % len(queues)], deps, name, dst[16 * k:16 * (k + 1), :], src[:, :])
        return (name, total[name])

    def relist(n, cv, of, dep):
        return [V([dep], vec.tensor_copy, of[:, 8 * k:8 * (k + 1)], cv[:, 2 * k + 1:16 * n:2 * n]) for k in range(n)]

    def gather(n, of, win, gt, deps):
        tk = []
        for t in (0, 1):
            tk.append(V(deps, vec.tensor_copy, gt[:, t:512 * n:4], win[:, K * t:K * (t + 1)].indirect(of[:, 0:8 * n])))
        for t in (2, 3):
            tk.append(S(deps, act, gt[:, t:512 * n:4], win[:, K * t:K * (t + 1)].indirect(of[:, 0:8 * n]), FN.Copy))
        return tk

    def give(group, cc, cs, dep, name, kc, ks, slot):
        send([dep], name, [([q], u8(cc, 128 * i, 128 * (i + 1)), u8(kc, 128 * slot(q), 128 * (slot(q) + 1)))
                           for i, q in enumerate(group)])
        send([dep], name, [([q], cs[:, 128 * i:128 * (i + 1)], ks[:, 128 * slot(q):128 * (slot(q) + 1)])
                           for i, q in enumerate(group)])

    def tell(group, mi, deps, name, sci):
        send(deps, name, [([q], mi[:, 2 * i:2 * i + 2], sci[:, 4 * me:4 * me + 2]) for i, q in enumerate(group)])

    def slot_a(q):
        return mates_of(q).index(me)

    def slot_b(q):
        return far_of(q).index(me)

    wx = 2 * width(1)
    ma = score(mates, [5, 6, 7], T.xqc, T.xqs, T.q1c, T.q1s, lambda q: ("ax%d" % q, wx), 0)
    mb = score(far, [0, 1, 2, 3], T.xqc, T.xqs, T.q1c, T.q1s, lambda q: ("ax%d" % q, wx), 0)
    sa = search(mates, [5, 6, 7], ma, T.mia)
    ca = spread("cva", T.mia, T.cva, sa, ["y"])
    tell(mates, T.mia, sa, "as1", T.sci1)
    sbt = search(far, [0, 1, 2, 3], mb, T.mib)
    cb = spread("cvb", T.mib, T.cvb, sbt, ["y", "s"])
    tell(far, T.mib, sbt, "as1", T.sci1)
    la = relist(3, T.cva, T.ofa, ca)
    ga = gather(3, T.ofa, T.c1p, T.gta, la + pl1)
    qa = V(ga, vec.quantize_mx, T.sac[:, :], T.sas[:, :], T.gta[:, :])
    give(mates, T.sac, T.sas, qa, "aka", T.kac, T.kas, slot_a)
    lb = relist(4, T.cvb, T.ofb, cb)
    gb = gather(4, T.ofb, T.c1p, T.gtb, lb + pl1)
    qb = V(gb, vec.quantize_mx, T.sbc[:, :], T.sbs[:, :], T.gtb[:, :])
    give(far, T.sbc, T.sbs, qb, "akb", T.kbc, T.kbs, slot_b)

    def choose(sci, pen, tp, pp, pos, mxo, deps):
        sc = sci[:, 0:32:4]
        a = V(deps, vec.tensor_reduce, mxo, sc, X, A.max)
        b = V([a], vec.tensor_scalar, pen[:, :], sc, mxo, BIG, A.is_lt, A.mult)
        c = V([b], vec.tensor_tensor, tp[:, :], pen[:, :], pp[:, :], A.add)
        return a, b, V([c], vec.tensor_reduce, pos[:, :], tp[:, :], X, A.min)

    def number(sci, num, pen, tn, wo, deps):
        a = V(deps, vec.tensor_tensor, num[:, :], sci[:, 1:32:4], T.nb[:, :], A.add)
        b = V([a], vec.tensor_tensor, tn[:, :], pen[:, :], num[:, :], A.add)
        return V([b], vec.tensor_reduce, wo, tn[:, :], X, A.min)

    po = V([n0, jv], vec.tensor_scalar, T.pp1[:, me:me + 1], T.sci1[:, 4 * me + 1:4 * me + 2], float(base1[me]), None, A.add)
    w4 = width(3)
    ars1 = ("as1", 3 * width(3) + 4 * width(4))
    c1a, c1b, c1c = choose(T.sci1, T.pen1, T.tp1, T.pp1, T.pos1, T.wp1[:, 1:2], [ars1, po, n0, wz] + p1 + ow)
    cp1 = spread("cvp1", T.pos1, T.cvp1, [c1c], ["y"])

    to2 = [mm(4 + b, K, T.eqc, T.eqs, 128 * b, T.q2c, T.q2s, hm, [q2, qe]) for b in range(4)]
    t2 = [[], [], [], []]

    def mate_table(b0, q, tks):
        for b in range(4):
            t2[b] += evac("v" if b < 2 else "s", b0 + b, K, T.tab2, W2, b, [(0, base2[q], K)], tks[b])

    mate_table(4, me, to2)
    da = [mm(b, 384, T.eqc, T.eqs, 128 * b, T.kac, T.kas, 0, [("aka", 2 * 3 * width(3)), qe]) for b in range(4)]
    pl2 = [V([d2], vec.tensor_copy, T.c2p[:, K * t:K * (t + 1)], T.c2t[:, t:4 * K:4]) for t in (0, 1)]
    pl2 += [S([d2], act, T.c2p[:, K * t:K * (t + 1)], T.c2t[:, t:4 * K:4], FN.Copy) for t in (2, 3)]
    ra = runs_of(mates, base1)
    for b in range(4):
        t1[b] += evac("v" if b < 2 else "s", b, 384, T.tab1, W1, b, ra, da[b])
    nu1 = number(T.sci1, T.num1, T.pen1, T.tn1, T.wp1[:, 0:1], [ars1, n0, i4, c1b, wz])
    wt = V([nu1, c1a], vec.transpose, T.wt1[:, :], T.wp1[:, :])
    of1 = V([cp1], vec.tensor_copy, T.ofp1[:, :], T.cvp1[:, :])

    db = [mm(4 + b, 512, T.eqc, T.eqs, 128 * b, T.kbc, T.kbs, 0, [("akb", 2 * 4 * width(4)), qe]) for b in range(4)]
    rb = runs_of(far, base1)
    for b in range(4):
        t1[b] += evac("v" if b < 1 else "s", 4 + b, 512, T.tab1, W1, b, rb, db[b])
    rr = [V([of1, xv] + t1[t], vec.tensor_tensor, T.rt[:, t:512:4], T.tab1[:, W1 * t:W1 * (t + 1)].indirect(T.ofp1[:, 0:8]),
            T.xv[:, t:512:4], A.add) for t in range(4)]
    qr = V(rr, vec.quantize_mx, T.rqc[:, m0:m0 + 128], T.rqs[:, m0:m0 + 128], T.rt[:, :])
    send([qr], "ar%d" % me, [(far, u8(T.rqc, m0, m0 + 128), u8(T.rqc, m0, m0 + 128))])
    send([qr], "ar%d" % me, [(far, T.rqs[:, m0:m0 + 128], T.rqs[:, m0:m0 + 128])])

    ac2 = ("ac2", 3 * 2 * width(1))
    ml = [mm(i, K, T.rqc, T.rqs, m0, T.q2c, T.q2s, K * i, [qr, q2, ac2]) for i in range(4)]
    m1 = [mm(4 + b, K, T.eqc, T.eqs, 128 * b, T.q2c, T.q2s, K * home.index(mates[0]), [ac2, qe]) for b in range(4)]
    sl = [scan(i, ml[i]) for i in range(4)]
    lo = []
    for (k, tk), q in zip(sl, home):
        lo.append(sign(k, tk, T.sci2[:, 4 * q + 1:4 * q + 2]))
    for (k, tk), q in zip(sl, home):
        lo.append(V([tk], vec.tensor_copy, T.sci2[:, 4 * q:4 * q + 1], T.run[:, K * (k + 1) - 1:K * (k + 1)]))
    rn = S(rr + [lr], act, T.rn[:, :], T.rt[:, 0:512].indirect(T.lrn[:, 0:32]), FN.Copy)
    mate_table(4, mates[0], m1)
    il = [D("y", [wt], "il", T.il[0:1, 128 * c:128 * (c + 1)], T.wt1[c:128:32, 0:32]) for c in range(2)]
    mc = score(far, [0, 1, 2, 3], T.rqc, T.rqs, T.q2c, T.q2s, lambda q: ("ar%d" % q, wx), hm)
    sct = search(far, [0, 1, 2, 3], mc, T.mic)
    cc = spread("cvc", T.mic, T.cvc, sct, ["y", "s"])
    tell(far, T.mic, sct, "as2", T.sci2)
    m2 = [mm(4 + b, K, T.eqc, T.eqs, 128 * b, T.q2c, T.q2s, K * home.index(mates[1]), [ac2, qe]) for b in range(4)]
    mate_table(4, mates[1], m2)
    lc = relist(4, T.cvc, T.ofc, cc)
    gc = gather(4, T.ofc, T.c2p, T.gtc, lc + pl2)
    qc = V(gc, vec.quantize_mx, T.scc[:, :], T.scs[:, :], T.gtc[:, :])
    give(far, T.scc, T.scs, qc, "akc", T.kcc, T.kcs, slot_b)

    p2 = []
    for q in ranks:
        if q in home:
            p2.append(V(lo, vec.tensor_scalar, T.pp2[:, q:q + 1], T.sci2[:, 4 * q + 1:4 * q + 2], float(base2[q]), None, A.add))
        else:
            p2.append(V([jv], vec.tensor_scalar, T.pp2[:, q:q + 1], T.jv[:, :], float(base2[q]), None, A.add))
    ars2 = ("as2", 4 * width(4))
    c2a, c2b, c2c = choose(T.sci2, T.pen2, T.tp2, T.pp2, T.pos2, T.wp2[:, 1:2], [ars2] + p2 + lo)
    cp2 = spread("cvp2", T.pos2, T.cvp2, [c2c], ["y"])
    nu2 = number(T.sci2, T.num2, T.pen2, T.tn2, T.wp2[:, 0:1], [ars2, i4, c2b] + lo)
    m3 = [mm(b, K, T.eqc, T.eqs, 128 * b, T.q2c, T.q2s, K * home.index(mates[2]), [ac2, qe]) for b in range(4)]
    mate_table(0, mates[2], m3)
    dn = D("y", [nu2, c2a, nz], "nc", T.nc[0:16, 0:16], T.wp2[:, :])
    ov = [V([il[1]], vec.tensor_copy, T.ou[0:1, 128 * c + h:128 * (c + 1):2], T.il[0:1, 128 * c + 64 * h:128 * c + 64 * (h + 1)])
          for c in range(2) for h in range(2)]
    D("y", ov, "no1", T.no[0:3:2, :], T.ou[0:1, :])
    of2 = V([cp2], vec.tensor_copy, T.ofp2[:, :], T.cvp2[:, :])
    nt = V([dn], vec.transpose, T.nct[0:32, :], T.nc[0:32, :])
    D("y", [nt], "no2", T.no[1, :], T.nct[0:16:2, 0:16])
    D("y", [nt], "no2", T.no[3, :], T.nct[1:16:2, 0:16])

    dc = [mm(4 + b, 512, T.eqc, T.eqs, 128 * b, T.kcc, T.kcs, 0, [("akc", 2 * 4 * width(4)), qe]) for b in range(4)]
    rc = runs_of(far, base2)
    for b in range(4):
        t2[b] += evac("v" if b < 1 else "s", 4 + b, 512, T.tab2, W2, b, rc, dc[b])
    yy = [V([of2, rn] + t2[t], vec.tensor_tensor, T.yt[:, t:512:4], T.tab2[:, W2 * t:W2 * (t + 1)].indirect(T.ofp2[:, 0:8]),
            T.rn[:, t:512:4], A.add) for t in range(4)]
    D("y", yy, "yo", T.y[:, :], T.yt[:, :])

    need("g", [(n, count[n]) for n in count] + [("ls", local[0])])
    need("y", [(n, total[n]) for n in total])
